import numpy as np
import ml_dtypes


def mxq(x, axis, fmt="e4m3"):
    dtype, down = {"e4m3": (ml_dtypes.float8_e4m3fn, 7), "e5m2": (ml_dtypes.float8_e5m2, 14)}[fmt]
    v = np.moveaxis(np.asarray(x, np.float32).astype(ml_dtypes.bfloat16).astype(np.float64), axis, -1)
    blocks = v.reshape(v.shape[:-1] + (-1, 32))
    amax = np.abs(blocks).max(-1, keepdims=True)
    byte = np.maximum(np.where(amax > 0, np.frexp(amax)[1] - 1 + 127, 0) - down, 1)
    scale = np.exp2(byte - 127.0)
    codes = (blocks / scale).astype(np.float32).astype(dtype).astype(np.float64)
    return np.moveaxis((codes * scale).reshape(v.shape), -1, axis)


WIDE = False


def mx_kscale(k):
    if not WIDE:
        return np.ones(k)
    levels = np.array([10, -10, 5, -5, 0])
    if k % 512:
        return np.exp2(np.random.permutation(np.resize(levels, k // 32))).repeat(32)
    a = np.empty((k // 512, 16))
    for p in range(k // 512):
        a[p, :8] = np.random.permutation(np.resize(levels, 8))
        for g in range(8):
            far = levels[np.abs(levels - a[p, g]) >= 10]
            a[p, g + 8] = far[np.random.randint(len(far))]
    return np.exp2(a.ravel()).repeat(32)


def f64(x):
    return np.asarray(x).astype(np.float64)


def striped(idx):
    return np.tile(np.asarray(idx).reshape(-1, 16).T, (8, 1)).astype(np.uint16)


def unstriped(offs):
    return offs[:16].T.reshape(-1).astype(np.int64)


E2M1 = np.array([0.0, 0.5, 1.0, 1.5, 2.0, 3.0, 4.0, 6.0, -0.0, -0.5, -1.0, -1.5, -2.0, -3.0, -4.0, -6.0])


def pack_weight(w, fmt):
    k, n = w.shape
    w = f64(np.asarray(w, np.float32).astype(ml_dtypes.bfloat16)).reshape(k // 32, 32, n)
    amax = np.abs(w).max(1)
    if fmt == "e4m3":
        byte = np.frexp(amax)[1] - 1 + 127 - 7
    else:
        mant, ex = np.frexp(amax / 6.0)
        byte = np.where(mant > 0.5, ex, ex - 1) + 127
    byte = np.clip(np.where(amax > 0, byte, 1), 1, 254)
    scaled = (w * np.exp2(127.0 - byte)[:, None, :]).reshape(k, n).astype(np.float32)
    by_word = np.ascontiguousarray(scaled.reshape(k // 512, 128, 4, n).transpose(0, 1, 3, 2))
    if fmt == "e4m3":
        words = by_word.astype(ml_dtypes.float8_e4m3fn).view(np.uint8)
    else:
        c = by_word.astype(ml_dtypes.float4_e2m1fn).view(np.uint8) & 0xF
        words = (c[..., 0::2] | (c[..., 1::2] << 4)).reshape(k // 512, 128, 2 * n)
    return np.ascontiguousarray(words), np.ascontiguousarray(byte.astype(np.uint8).reshape(k // 512, 16, n))


def unpack_weight(words, scales, fmt):
    g, _, n = scales.shape
    words = np.ascontiguousarray(words).reshape(g, 128, n, -1)
    if fmt == "e4m3":
        vals = words.view(ml_dtypes.float8_e4m3fn).astype(np.float64)
    else:
        nib = np.empty((g, 128, n, 4), np.uint8)
        nib[..., 0::2] = words & 0xF
        nib[..., 1::2] = words >> 4
        vals = E2M1[nib]
    vals = vals * np.repeat(np.exp2(scales.astype(np.float64) - 127.0), 8, axis=1)[..., None]
    return vals.transpose(0, 1, 3, 2).reshape(g * 512, n)


D, E, T, I, Q, G = 512, 512, 2048, 512, 128, 64


def setup_inputs():
    n = np.random.standard_normal
    idx = np.random.permutation(T)[:I]
    fd = mx_kscale(D)
    fe = mx_kscale(E)
    keysp = pack_weight(n((D, T)) / fd[:, None], "e4m3")
    valsp = pack_weight(n((E, T)) / fe[:, None], "e4m3")
    return {
        "query": (n((D, Q)) * 0.8 / np.sqrt(D) * fd[:, None]).astype(np.float32),
        "query2": (n((D, Q)) * 0.8 / np.sqrt(D) * fd[:, None]).astype(np.float32),
        "keys_words": keysp[0],
        "keys_scales": keysp[1],
        "gout": (n((E, Q)) * 1 / np.sqrt(E) * fe[:, None]).astype(np.float32),
        "vals_words": valsp[0],
        "vals_scales": valsp[1],
        "old": (0.5 * n((Q, T))).astype(np.float32),
        "offs": striped(idx),
    }


def reference(query, query2, keys_words, keys_scales, gout, vals_words, vals_scales, old, offs):
    idx = unstriped(offs)
    keysu = unpack_weight(keys_words, keys_scales, "e4m3")
    valsu = unpack_weight(vals_words, vals_scales, "e4m3")
    queryq = mxq(f64(query), 0, "e4m3")
    keysidxg = keysu[:, idx]
    a = queryq.T @ keysidxg
    query2q = mxq(f64(query2), 0, "e4m3")
    b = query2q.T @ keysidxg
    pa = np.exp(a)
    sa = pa.reshape(Q, G, I // G).sum(axis=2)
    z = np.sum(sa, axis=1, keepdims=True)
    pb = np.exp(b)
    sb = pb.reshape(Q, G, I // G).sum(axis=2)
    goutq = mxq(f64(gout), 0, "e4m3")
    valsidxg = valsu[:, idx]
    c0 = goutq.T @ valsidxg
    drr = c0 * pb
    dr = drr.reshape(Q, G, I // G).sum(axis=2)
    dz = np.sum(dr / sb * sa / np.square(z) * (-1.0), axis=1, keepdims=True)
    dsa = dr / sb / z + dz
    r1 = np.repeat(dsa, I // G, axis=1)
    da = r1 * pa
    gs = da * 512.0
    gf = np.zeros((Q, T))
    gf[:, idx] = gs
    y = f64(old) + gf
    return y

@@ -1,0 +1,150 @@
+from contextlib import ExitStack
+
+import concourse.mybir as mybir
+
+F32 = mybir.dt.float32
+BF16 = mybir.dt.bfloat16
+I32 = mybir.dt.int32
+U32 = mybir.dt.uint32
+U16 = mybir.dt.uint16
+U8 = mybir.dt.uint8
+FP8X4 = mybir.dt.float8_e4m3fn_x4
+ALU = mybir.AluOpType
+ACT = mybir.ActivationFunctionType
+AX = mybir.AxisListType
+
+P = 128
+PACK = 4
+T = 2048
+SLOTS = 512
+Q = 128
+PAGES = 64
+PAGE = SLOTS // PAGES
+GAIN = 512.0
+VALS_PLANE = 4
+OUT_CHUNK = 512
+
+FLOPS = 3 * 2 * 512 * Q * SLOTS
+
+
+def tile_attend_bpagethensecond_s_kernel(tc, query, query2, keys_words, keys_scales, gout, vals_words, vals_scales, old, offs, out):
+    nc = tc.nc
+    with ExitStack() as ctx:
+        keep = ctx.enter_context(tc.tile_pool(name="keep", bufs=1))
+        psum = ctx.enter_context(tc.psum_pool(name="psum", bufs=1))
+
+        def load_scales(queue, window, scales, first):
+            rows = scales[0].bitcast(I32)
+            for r in range(4):
+                queue.dma_start(window[:].bitcast(I32)[first + r : P : 32, :], rows[r:16:4, :])
+
+        def load_words(window, words):
+            nc.sync.dma_start(window[:], words[0].rearrange("p t r -> p (t r)").bitcast(I32))
+
+        def load_rows(raw, rows):
+            nc.sync.dma_start(raw[:], rows.rearrange("(p j) w -> p j w", j=PACK))
+
+        def quantize(raw, name):
+            grouped = keep.tile([P, Q, PACK], BF16, align_bytes=64, name=name + "_grouped")
+            nc.scalar.copy(grouped[:], raw[:].rearrange("p j w -> p w j"))
+            codes = keep.tile([P, Q], U32, align_bytes=64, name=name + "_codes")
+            plane = keep.tile([P, Q], U8, align_bytes=64, name=name + "_plane")
+            nc.vector.quantize_mx(out=codes[:].bitcast(FP8X4), scales=plane[:], in_=grouped[:].rearrange("p w j -> p (w j)"))
+            return codes, plane
+
+        def gather(window, dtype, name):
+            picked = keep.tile([P, SLOTS], dtype, align_bytes=64, name=name)
+            nc.vector.tensor_copy(picked[:], window.indirect(offsets[:]))
+            return picked
+
+        def product(codes, plane, words, scales, name):
+            bank = psum.tile([P, SLOTS], F32, name=name)
+            nc.tensor.matmul_mx(out=bank[:], lhsT=codes[:].bitcast(FP8X4), lhsT_scale=plane[:], rhs=words[:].bitcast(FP8X4), rhs_scale=scales, start=True, stop=True)
+            return bank
+
+        def by_page(ap):
+            return ap.rearrange("p (g j) -> p g j", j=PAGE)
+
+        def over_page(ap):
+            return ap.unsqueeze(2).to_broadcast([P, PAGES, PAGE])
+
+        ks_window = keep.tile([P, T], U8)
+        vs_window = keep.tile([P, T], U8)
+        nc.vector.memset(ks_window[:].bitcast(I32), 0)
+        nc.vector.memset(vs_window[:].bitcast(I32), 0)
+        warm_in = keep.tile([P, 1], F32)
+        warm_out = keep.tile([P, 1], F32)
+        nc.vector.memset(warm_in[:], 0.0)
+        placed = keep.tile([P, T], F32)
+        nc.vector.memset(placed[:], 0.0)
+
+        offsets = keep.tile([P, SLOTS // 16], U16)
+        nc.sync.dma_start(offsets[:], offs)
+        load_scales(nc.scalar, ks_window, keys_scales, 0)
+        load_scales(nc.gpsimd, vs_window, vals_scales, VALS_PLANE)
+        nc.scalar.activation(warm_out[:], warm_in[:], ACT.Exp)
+        q2_raw = keep.tile([P, PACK, Q], F32, tag="chain_a")
+        load_rows(q2_raw, query2)
+        kw_window = keep.tile([P, T], I32)
+        load_words(kw_window, keys_words)
+        q_raw = keep.tile([P, PACK, Q], F32, tag="chain_b")
+        load_rows(q_raw, query)
+
+        ks = gather(ks_window[:], U8, "ks")
+        q2_codes, q2_plane = quantize(q2_raw, "q2")
+        vw_window = keep.tile([P, T], I32, tag="chain_a")
+        load_words(vw_window, vals_words)
+        kw = gather(kw_window[:].bitcast(U32), U32, "kw")
+        b = product(q2_codes, q2_plane, kw, ks[:], "b")
+        q_codes, q_plane = quantize(q_raw, "q")
+        g_raw = keep.tile([P, PACK, Q], F32, tag="chain_b")
+        load_rows(g_raw, gout)
+        a = product(q_codes, q_plane, kw, ks[:], "a")
+        vs = gather(vs_window[:], U8, "vs")
+
+        neg_b_max = keep.tile([P, PAGES], F32)
+        nc.vector.tensor_reduce(neg_b_max[:], by_page(b[:]), AX.X, ALU.max, negate=True)
+        neg_a_max = keep.tile([P, 1], F32)
+        nc.vector.tensor_reduce(neg_a_max[:], a[:], AX.X, ALU.max, negate=True)
+        b_shifted = keep.tile([P, SLOTS], F32)
+        nc.vector.tensor_tensor(by_page(b_shifted[:]), by_page(b[:]), over_page(neg_b_max[:]), ALU.add)
+        sums = keep.tile([P, PAGES + 1], F32)
+        pa = keep.tile([P, SLOTS], F32)
+        nc.scalar.activation(pa[:], a[:], ACT.Exp, bias=neg_a_max[:], accum_out=sums[:, PAGES : PAGES + 1])
+        pb = keep.tile([P, SLOTS], F32)
+        nc.scalar.activation(pb[:], b_shifted[:], ACT.Exp)
+
+        vw = gather(vw_window[:].bitcast(U32), U32, "vw")
+        g_codes, g_plane = quantize(g_raw, "g")
+        old_sb = keep.tile([P, T], F32, tag="chain_a")
+        nc.sync.dma_start(old_sb[:], old)
+        c0 = product(g_codes, g_plane, vw, vs[VALS_PLANE:P, :], "c0")
+
+        nc.vector.tensor_reduce(sums[:, 0:PAGES], by_page(pb[:]), AX.X, ALU.add)
+        sa = keep.tile([P, PAGES], F32)
+        nc.vector.tensor_reduce(sa[:], by_page(pa[:]), AX.X, ALU.add)
+        inv = keep.tile([P, PAGES + 1], F32)
+        nc.vector.reciprocal(inv[:], sums[:])
+        inv_z = inv[:, PAGES : PAGES + 1]
+        drr = keep.tile([P, SLOTS], F32)
+        nc.vector.tensor_tensor(drr[:], c0[:], pb[:], ALU.mult)
+        page_gain = keep.tile([P, PAGES], F32)
+        nc.vector.tensor_scalar(page_gain[:], inv[:, 0:PAGES], inv_z, GAIN, ALU.mult, ALU.mult)
+        dr = keep.tile([P, PAGES], F32)
+        nc.vector.tensor_reduce(dr[:], by_page(drr[:]), AX.X, ALU.add)
+        mean_gain = keep.tile([P, PAGES], F32)
+        nc.vector.scalar_tensor_tensor(mean_gain[:], sa[:], inv_z, page_gain[:], ALU.mult, ALU.mult)
+        page_term = keep.tile([P, PAGES], F32)
+        nc.vector.tensor_tensor(page_term[:], dr[:], page_gain[:], ALU.mult)
+        mean_terms = keep.tile([P, PAGES], F32)
+        mean = keep.tile([P, 1], F32)
+        nc.vector.scalar_tensor_tensor(mean_terms[:], dr[:], 1.0, mean_gain[:], ALU.mult, ALU.mult, accum_out=mean[:])
+        spread = keep.tile([P, SLOTS], F32)
+        nc.vector.tensor_scalar(by_page(spread[:]), over_page(page_term[:]), mean[:], None, ALU.subtract)
+        nc.vector.tensor_tensor(placed[:].indirect(offsets[:]), spread[:], pa[:], ALU.mult)
+
+        for c in range(T // OUT_CHUNK):
+            cols = slice(c * OUT_CHUNK, (c + 1) * OUT_CHUNK)
+            result = keep.tile([P, OUT_CHUNK], F32, name="result%d" % c)
+            nc.vector.tensor_tensor(result[:], placed[:, cols], old_sb[:, cols], ALU.add)
+            nc.sync.dma_start(out[:, cols], result[:])

@@ -1,6 +1,7 @@
 from contextlib import ExitStack
 
 import concourse.mybir as mybir
+from concourse.masks import make_identity
 
 F32 = mybir.dt.float32
 BF16 = mybir.dt.bfloat16
@@ -21,8 +22,7 @@ Q = 128
 PAGES = 64
 PAGE = SLOTS // PAGES
 GAIN = 512.0
-VALS_PLANE = 4
-OUT_CHUNK = 512
+HALF = SLOTS // 2
 
 FLOPS = 3 * 2 * 512 * Q * SLOTS
 
@@ -33,10 +33,18 @@ def tile_attend_bpagethensecond_s_kernel(tc, query, query2, keys_words, keys_sca
         keep = ctx.enter_context(tc.tile_pool(name="keep", bufs=1))
         psum = ctx.enter_context(tc.psum_pool(name="psum", bufs=1))
 
-        def load_scales(queue, window, scales, first):
-            rows = scales[0].bitcast(I32)
-            for r in range(4):
-                queue.dma_start(window[:].bitcast(I32)[first + r : P : 32, :], rows[r:16:4, :])
+        def load_scales(window, scales, first):
+            rows = scales[0].bitcast(I32).unsqueeze(1).to_broadcast([16, 2, T // 4])
+            nc.sync.dma_start(window[:].bitcast(I32)[first : first + 32, :], rows)
+
+        def place_scales(picked, first, name):
+            plane = keep.tile([P, SLOTS], U8, align_bytes=64, name=name)
+            for quad in range(4):
+                nc.sync.dma_start(
+                    plane[:].bitcast(I32)[32 * quad : 32 * quad + 4, :],
+                    picked[:].bitcast(I32)[first + 8 * quad : first + 8 * quad + 8 : 2, :],
+                )
+            return plane
 
         def load_words(window, words):
             nc.sync.dma_start(window[:], words[0].rearrange("p t r -> p (t r)").bitcast(I32))
@@ -58,93 +66,119 @@ def tile_attend_bpagethensecond_s_kernel(tc, query, query2, keys_words, keys_sca
             return picked
 
         def product(codes, plane, words, scales, name):
-            bank = psum.tile([P, SLOTS], F32, name=name)
-            nc.tensor.matmul_mx(out=bank[:], lhsT=codes[:].bitcast(FP8X4), lhsT_scale=plane[:], rhs=words[:].bitcast(FP8X4), rhs_scale=scales, start=True, stop=True)
+            bank = psum.tile([P, words.shape[1]], F32, name=name)
+            nc.tensor.matmul_mx(out=bank[:], lhsT=codes[:].bitcast(FP8X4), lhsT_scale=plane[:], rhs=words.bitcast(FP8X4), rhs_scale=scales, start=True, stop=True)
             return bank
 
         def by_page(ap):
             return ap.rearrange("p (g j) -> p g j", j=PAGE)
 
         def over_page(ap):
-            return ap.unsqueeze(2).to_broadcast([P, PAGES, PAGE])
+            return ap.unsqueeze(2).to_broadcast([P, ap.shape[1], PAGE])
 
-        ks_window = keep.tile([P, T], U8)
-        vs_window = keep.tile([P, T], U8)
-        nc.vector.memset(ks_window[:].bitcast(I32), 0)
-        nc.vector.memset(vs_window[:].bitcast(I32), 0)
+        ks_window = keep.tile([P, T], U8, tag="chain_a")
+        vs_window = keep.tile([P, T], U8, tag="chain_b")
+        nc.vector.memset(ks_window[:].bitcast(I32)[32:64, :], 0)
+        nc.vector.memset(ks_window[:].bitcast(I32)[64:128, :], 0)
+        nc.vector.memset(vs_window[:].bitcast(I32)[0:64, :], 0)
+        nc.vector.memset(vs_window[:].bitcast(I32)[96:128, :], 0)
         warm_in = keep.tile([P, 1], F32)
         warm_out = keep.tile([P, 1], F32)
         nc.vector.memset(warm_in[:], 0.0)
         placed = keep.tile([P, T], F32)
         nc.vector.memset(placed[:], 0.0)
+        identity = keep.tile([P, P], F32)
+        make_identity(nc, identity[:])
 
         offsets = keep.tile([P, SLOTS // 16], U16)
         nc.sync.dma_start(offsets[:], offs)
-        load_scales(nc.scalar, ks_window, keys_scales, 0)
-        load_scales(nc.gpsimd, vs_window, vals_scales, VALS_PLANE)
-        nc.scalar.activation(warm_out[:], warm_in[:], ACT.Exp)
-        q2_raw = keep.tile([P, PACK, Q], F32, tag="chain_a")
+        load_scales(ks_window, keys_scales, 0)
+        load_scales(vs_window, vals_scales, 64)
+        q2_raw = keep.tile([P, PACK, Q], F32)
         load_rows(q2_raw, query2)
-        kw_window = keep.tile([P, T], I32)
+        kw_window = keep.tile([P, T], I32, tag="chain_c")
         load_words(kw_window, keys_words)
-        q_raw = keep.tile([P, PACK, Q], F32, tag="chain_b")
+        q_raw = keep.tile([P, PACK, Q], F32)
         load_rows(q_raw, query)
+        nc.scalar.activation(warm_out[:], warm_in[:], ACT.Exp)
 
-        ks = gather(ks_window[:], U8, "ks")
-        q2_codes, q2_plane = quantize(q2_raw, "q2")
-        vw_window = keep.tile([P, T], I32, tag="chain_a")
-        load_words(vw_window, vals_words)
-        kw = gather(kw_window[:].bitcast(U32), U32, "kw")
-        b = product(q2_codes, q2_plane, kw, ks[:], "b")
-        q_codes, q_plane = quantize(q_raw, "q")
-        g_raw = keep.tile([P, PACK, Q], F32, tag="chain_b")
+        ks_rows = gather(ks_window[:], U8, "ks_rows")
+        ks = place_scales(ks_rows, 0, "ks")
+        vs_rows = gather(vs_window[:], U8, "vs_rows")
+        g_raw = keep.tile([P, PACK, Q], F32, tag="chain_a")
         load_rows(g_raw, gout)
-        a = product(q_codes, q_plane, kw, ks[:], "a")
-        vs = gather(vs_window[:], U8, "vs")
+        vw_window = keep.tile([P, T], I32, tag="chain_b")
+        load_words(vw_window, vals_words)
+        vs = place_scales(vs_rows, 64, "vs")
+        q2_codes, q2_plane = quantize(q2_raw, "q2")
+
+        kw = keep.tile([P, SLOTS], U32, align_bytes=64)
+        halves = [slice(h * HALF, (h + 1) * HALF) for h in range(2)]
+        half_pages = [slice(h * HALF // PAGE, (h + 1) * HALF // PAGE) for h in range(2)]
+        b = []
+        for h in range(2):
+            nc.vector.tensor_copy(kw[:, halves[h]], kw_window[:].bitcast(U32).indirect(offsets[:, h * HALF // 16 : (h + 1) * HALF // 16]))
+            b.append(product(q2_codes, q2_plane, kw[:, halves[h]], ks[:, halves[h]], "b%d" % h))
+        old_sb = keep.tile([P, T], F32, tag="chain_c")
+        nc.sync.dma_start(old_sb[:], old)
+        q_codes, q_plane = quantize(q_raw, "q")
+        a = product(q_codes, q_plane, kw[:], ks[:], "a")
+        g_codes, g_plane = quantize(g_raw, "g")
 
         neg_b_max = keep.tile([P, PAGES], F32)
-        nc.vector.tensor_reduce(neg_b_max[:], by_page(b[:]), AX.X, ALU.max, negate=True)
+        for h in range(2):
+            nc.vector.tensor_reduce(neg_b_max[:, half_pages[h]], by_page(b[h][:]), AX.X, ALU.max, negate=True)
+        b_shifted = keep.tile([P, SLOTS], F32)
+        for h in range(2):
+            nc.vector.tensor_tensor(by_page(b_shifted[:, halves[h]]), by_page(b[h][:]), over_page(neg_b_max[:, half_pages[h]]), ALU.add)
         neg_a_max = keep.tile([P, 1], F32)
         nc.vector.tensor_reduce(neg_a_max[:], a[:], AX.X, ALU.max, negate=True)
-        b_shifted = keep.tile([P, SLOTS], F32)
-        nc.vector.tensor_tensor(by_page(b_shifted[:]), by_page(b[:]), over_page(neg_b_max[:]), ALU.add)
         sums = keep.tile([P, PAGES + 1], F32)
+        pb = keep.tile([P, SLOTS], F32, tag="chain_a")
+        nc.scalar.activation(pb[:], b_shifted[:], ACT.Exp)
         pa = keep.tile([P, SLOTS], F32)
         nc.scalar.activation(pa[:], a[:], ACT.Exp, bias=neg_a_max[:], accum_out=sums[:, PAGES : PAGES + 1])
-        pb = keep.tile([P, SLOTS], F32)
-        nc.scalar.activation(pb[:], b_shifted[:], ACT.Exp)
+        nc.vector.tensor_reduce(sums[:, 0:PAGES], by_page(pb[:]), AX.X, ALU.add)
+
+        turned = psum.tile([P, P], F32)
+        for t in range(4):
+            nc.tensor.matmul(turned[:], lhsT=pa[:, t:SLOTS:4], rhs=identity[:], is_transpose=True, start=(t == 0), stop=(t == 3))
+        turned_sb = keep.tile([P, P], F32)
+        nc.scalar.copy(turned_sb[:], turned[:])
+        sa_halves = psum.tile([P, P], F32)
+        nc.tensor.transpose(sa_halves[:], turned_sb[:], identity[:])
 
         vw = gather(vw_window[:].bitcast(U32), U32, "vw")
-        g_codes, g_plane = quantize(g_raw, "g")
-        old_sb = keep.tile([P, T], F32, tag="chain_a")
-        nc.sync.dma_start(old_sb[:], old)
-        c0 = product(g_codes, g_plane, vw, vs[VALS_PLANE:P, :], "c0")
+        c0 = product(g_codes, g_plane, vw[:], vs[:], "c0")
 
-        nc.vector.tensor_reduce(sums[:, 0:PAGES], by_page(pb[:]), AX.X, ALU.add)
-        sa = keep.tile([P, PAGES], F32)
-        nc.vector.tensor_reduce(sa[:], by_page(pa[:]), AX.X, ALU.add)
-        inv = keep.tile([P, PAGES + 1], F32)
+        inv = keep.tile([P, PAGES + 1], F32, tag="chain_b")
         nc.vector.reciprocal(inv[:], sums[:])
         inv_z = inv[:, PAGES : PAGES + 1]
-        drr = keep.tile([P, SLOTS], F32)
-        nc.vector.tensor_tensor(drr[:], c0[:], pb[:], ALU.mult)
         page_gain = keep.tile([P, PAGES], F32)
         nc.vector.tensor_scalar(page_gain[:], inv[:, 0:PAGES], inv_z, GAIN, ALU.mult, ALU.mult)
+        drr = keep.tile([P, SLOTS], F32)
+        nc.vector.tensor_tensor(drr[:], c0[:], pb[:], ALU.mult)
         dr = keep.tile([P, PAGES], F32)
         nc.vector.tensor_reduce(dr[:], by_page(drr[:]), AX.X, ALU.add)
-        mean_gain = keep.tile([P, PAGES], F32)
-        nc.vector.scalar_tensor_tensor(mean_gain[:], sa[:], inv_z, page_gain[:], ALU.mult, ALU.mult)
         page_term = keep.tile([P, PAGES], F32)
         nc.vector.tensor_tensor(page_term[:], dr[:], page_gain[:], ALU.mult)
-        mean_terms = keep.tile([P, PAGES], F32)
+        mean_terms = keep.tile([P, PAGES, 2], F32)
         mean = keep.tile([P, 1], F32)
-        nc.vector.scalar_tensor_tensor(mean_terms[:], dr[:], 1.0, mean_gain[:], ALU.mult, ALU.mult, accum_out=mean[:])
+        nc.vector.scalar_tensor_tensor(
+            mean_terms[:],
+            sa_halves[:].rearrange("p (g h) -> p g h", h=2),
+            inv_z,
+            page_term[:].unsqueeze(2).to_broadcast([P, PAGES, 2]),
+            ALU.mult,
+            ALU.mult,
+            accum_out=mean[:],
+        )
         spread = keep.tile([P, SLOTS], F32)
         nc.vector.tensor_scalar(by_page(spread[:]), over_page(page_term[:]), mean[:], None, ALU.subtract)
         nc.vector.tensor_tensor(placed[:].indirect(offsets[:]), spread[:], pa[:], ALU.mult)
 
-        for c in range(T // OUT_CHUNK):
-            cols = slice(c * OUT_CHUNK, (c + 1) * OUT_CHUNK)
-            result = keep.tile([P, OUT_CHUNK], F32, name="result%d" % c)
+        for c, (lo, hi) in enumerate(((0, 256), (256, 768), (768, 1280), (1280, 1792), (1792, 2048))):
+            cols = slice(lo, hi)
+            result = keep.tile([P, hi - lo], F32, name="result%d" % c)
             nc.vector.tensor_tensor(result[:], placed[:, cols], old_sb[:, cols], ALU.add)
             nc.sync.dma_start(out[:, cols], result[:])

@@ -23,6 +23,7 @@ PAGES = 64
 PAGE = SLOTS // PAGES
 GAIN = 512.0
 HALF = SLOTS // 2
+ROWS_AT = P - 16
 
 FLOPS = 3 * 2 * 512 * Q * SLOTS
 
@@ -33,16 +34,16 @@ def tile_attend_bpagethensecond_s_kernel(tc, query, query2, keys_words, keys_sca
         keep = ctx.enter_context(tc.tile_pool(name="keep", bufs=1))
         psum = ctx.enter_context(tc.psum_pool(name="psum", bufs=1))
 
-        def load_scales(window, scales, first):
-            rows = scales[0].bitcast(I32).unsqueeze(1).to_broadcast([16, 2, T // 4])
-            nc.sync.dma_start(window[:].bitcast(I32)[first : first + 32, :], rows)
+        def load_scales(window, scales):
+            nc.vector.memset(window[:].bitcast(I32)[0:ROWS_AT, :], 0)
+            nc.sync.dma_start(window[:].bitcast(I32)[ROWS_AT:P, :], scales[0].bitcast(I32))
 
-        def place_scales(picked, first, name):
+        def place_scales(picked, name):
             plane = keep.tile([P, SLOTS], U8, align_bytes=64, name=name)
             for quad in range(4):
                 nc.sync.dma_start(
                     plane[:].bitcast(I32)[32 * quad : 32 * quad + 4, :],
-                    picked[:].bitcast(I32)[first + 8 * quad : first + 8 * quad + 8 : 2, :],
+                    picked[:].bitcast(I32)[ROWS_AT + 4 * quad : ROWS_AT + 4 * quad + 4, :],
                 )
             return plane
 
@@ -77,11 +78,11 @@ def tile_attend_bpagethensecond_s_kernel(tc, query, query2, keys_words, keys_sca
             return ap.unsqueeze(2).to_broadcast([P, ap.shape[1], PAGE])
 
         ks_window = keep.tile([P, T], U8, tag="chain_a")
-        vs_window = keep.tile([P, T], U8, tag="chain_b")
-        nc.vector.memset(ks_window[:].bitcast(I32)[32:64, :], 0)
-        nc.vector.memset(ks_window[:].bitcast(I32)[64:128, :], 0)
-        nc.vector.memset(vs_window[:].bitcast(I32)[0:64, :], 0)
-        nc.vector.memset(vs_window[:].bitcast(I32)[96:128, :], 0)
+        vs_window = keep.tile([P, T], U8)
+        offsets = keep.tile([P, SLOTS // 16], U16)
+        nc.sync.dma_start(offsets[:], offs)
+        load_scales(ks_window, keys_scales)
+        load_scales(vs_window, vals_scales)
         warm_in = keep.tile([P, 1], F32)
         warm_out = keep.tile([P, 1], F32)
         nc.vector.memset(warm_in[:], 0.0)
@@ -90,11 +91,7 @@ def tile_attend_bpagethensecond_s_kernel(tc, query, query2, keys_words, keys_sca
         identity = keep.tile([P, P], F32)
         make_identity(nc, identity[:])
 
-        offsets = keep.tile([P, SLOTS // 16], U16)
-        nc.sync.dma_start(offsets[:], offs)
-        load_scales(ks_window, keys_scales, 0)
-        load_scales(vs_window, vals_scales, 64)
-        q2_raw = keep.tile([P, PACK, Q], F32)
+        q2_raw = keep.tile([P, PACK, Q], F32, tag="chain_b")
         load_rows(q2_raw, query2)
         kw_window = keep.tile([P, T], I32, tag="chain_c")
         load_words(kw_window, keys_words)
@@ -103,14 +100,14 @@ def tile_attend_bpagethensecond_s_kernel(tc, query, query2, keys_words, keys_sca
         nc.scalar.activation(warm_out[:], warm_in[:], ACT.Exp)
 
         ks_rows = gather(ks_window[:], U8, "ks_rows")
-        ks = place_scales(ks_rows, 0, "ks")
+        ks = place_scales(ks_rows, "ks")
         vs_rows = gather(vs_window[:], U8, "vs_rows")
+        q2_codes, q2_plane = quantize(q2_raw, "q2")
         g_raw = keep.tile([P, PACK, Q], F32, tag="chain_a")
         load_rows(g_raw, gout)
         vw_window = keep.tile([P, T], I32, tag="chain_b")
         load_words(vw_window, vals_words)
-        vs = place_scales(vs_rows, 64, "vs")
-        q2_codes, q2_plane = quantize(q2_raw, "q2")
+        vs = place_scales(vs_rows, "vs")
 
         kw = keep.tile([P, SLOTS], U32, align_bytes=64)
         halves = [slice(h * HALF, (h + 1) * HALF) for h in range(2)]
@@ -129,46 +126,64 @@ def tile_attend_bpagethensecond_s_kernel(tc, query, query2, keys_words, keys_sca
         for h in range(2):
             nc.vector.tensor_reduce(neg_b_max[:, half_pages[h]], by_page(b[h][:]), AX.X, ALU.max, negate=True)
         b_shifted = keep.tile([P, SLOTS], F32)
+        neg_a_max = keep.tile([P, 1], F32)
         for h in range(2):
             nc.vector.tensor_tensor(by_page(b_shifted[:, halves[h]]), by_page(b[h][:]), over_page(neg_b_max[:, half_pages[h]]), ALU.add)
-        neg_a_max = keep.tile([P, 1], F32)
-        nc.vector.tensor_reduce(neg_a_max[:], a[:], AX.X, ALU.max, negate=True)
-        sums = keep.tile([P, PAGES + 1], F32)
-        pb = keep.tile([P, SLOTS], F32, tag="chain_a")
+            if h == 0:
+                nc.vector.tensor_reduce(neg_a_max[:], a[:], AX.X, ALU.max, negate=True)
+        z = keep.tile([P, 1], F32)
+        pa = keep.tile([P, SLOTS], F32, tag="chain_a")
+        nc.scalar.activation(pa[:], a[:], ACT.Exp, bias=neg_a_max[:], accum_out=z[:])
+        pb = keep.tile([P, SLOTS], F32)
         nc.scalar.activation(pb[:], b_shifted[:], ACT.Exp)
-        pa = keep.tile([P, SLOTS], F32)
-        nc.scalar.activation(pa[:], a[:], ACT.Exp, bias=neg_a_max[:], accum_out=sums[:, PAGES : PAGES + 1])
-        nc.vector.tensor_reduce(sums[:, 0:PAGES], by_page(pb[:]), AX.X, ALU.add)
 
         turned = psum.tile([P, P], F32)
         for t in range(4):
             nc.tensor.matmul(turned[:], lhsT=pa[:, t:SLOTS:4], rhs=identity[:], is_transpose=True, start=(t == 0), stop=(t == 3))
-        turned_sb = keep.tile([P, P], F32)
+
+        c0 = []
+        for h in range(2):
+            vw = keep.tile([P, HALF], U32, align_bytes=64, name="vw%d" % h)
+            nc.vector.tensor_copy(vw[:], vw_window[:].bitcast(U32).indirect(offsets[:, h * HALF // 16 : (h + 1) * HALF // 16]))
+            c0.append(product(g_codes, g_plane, vw[:], vs[:, halves[h]], "c%d" % h))
+
+        turned_sb = keep.tile([P, P], F32, align_bytes=64, name="vw1")
         nc.scalar.copy(turned_sb[:], turned[:])
         sa_halves = psum.tile([P, P], F32)
         nc.tensor.transpose(sa_halves[:], turned_sb[:], identity[:])
 
-        vw = gather(vw_window[:].bitcast(U32), U32, "vw")
-        c0 = product(g_codes, g_plane, vw[:], vs[:], "c0")
-
-        inv = keep.tile([P, PAGES + 1], F32, tag="chain_b")
-        nc.vector.reciprocal(inv[:], sums[:])
-        inv_z = inv[:, PAGES : PAGES + 1]
-        page_gain = keep.tile([P, PAGES], F32)
-        nc.vector.tensor_scalar(page_gain[:], inv[:, 0:PAGES], inv_z, GAIN, ALU.mult, ALU.mult)
+        sb = keep.tile([P, PAGES], F32, align_bytes=64, name="vw0")
+        nc.vector.tensor_reduce(sb[:], by_page(pb[:]), AX.X, ALU.add)
+        inv_z_tile = keep.tile([P, 1], F32, align_bytes=64, name="g_codes")
+        nc.vector.reciprocal(inv_z_tile[:], z[:])
+        inv_z = inv_z_tile[:]
         drr = keep.tile([P, SLOTS], F32)
-        nc.vector.tensor_tensor(drr[:], c0[:], pb[:], ALU.mult)
+        nc.vector.tensor_tensor(drr[:, halves[0]], c0[0][:], pb[:, halves[0]], ALU.mult)
+        inv_sb = keep.tile([P, PAGES], F32)
+        nc.vector.reciprocal(inv_sb[:], sb[:])
+        nc.vector.tensor_tensor(drr[:, halves[1]], c0[1][:], pb[:, halves[1]], ALU.mult)
+        page_gain = keep.tile([P, PAGES], F32)
+        nc.vector.tensor_scalar(page_gain[:], inv_sb[:], inv_z, GAIN, ALU.mult, ALU.mult)
         dr = keep.tile([P, PAGES], F32)
         nc.vector.tensor_reduce(dr[:], by_page(drr[:]), AX.X, ALU.add)
+        mean_gain = keep.tile([P, PAGES, 2], F32)
+        nc.vector.scalar_tensor_tensor(
+            mean_gain[:],
+            sa_halves[:].rearrange("p (g h) -> p g h", h=2),
+            inv_z,
+            page_gain[:].unsqueeze(2).to_broadcast([P, PAGES, 2]),
+            ALU.mult,
+            ALU.mult,
+        )
         page_term = keep.tile([P, PAGES], F32)
         nc.vector.tensor_tensor(page_term[:], dr[:], page_gain[:], ALU.mult)
         mean_terms = keep.tile([P, PAGES, 2], F32)
         mean = keep.tile([P, 1], F32)
         nc.vector.scalar_tensor_tensor(
             mean_terms[:],
-            sa_halves[:].rearrange("p (g h) -> p g h", h=2),
-            inv_z,
-            page_term[:].unsqueeze(2).to_broadcast([P, PAGES, 2]),
+            mean_gain[:],
+            1.0,
+            dr[:].unsqueeze(2).to_broadcast([P, PAGES, 2]),
             ALU.mult,
             ALU.mult,
             accum_out=mean[:],

from contextlib import ExitStack

import concourse.mybir as mybir
from concourse.masks import make_identity

F32 = mybir.dt.float32
BF16 = mybir.dt.bfloat16
I32 = mybir.dt.int32
U32 = mybir.dt.uint32
U16 = mybir.dt.uint16
U8 = mybir.dt.uint8
FP8X4 = mybir.dt.float8_e4m3fn_x4
ALU = mybir.AluOpType
ACT = mybir.ActivationFunctionType
AX = mybir.AxisListType

P = 128
PACK = 4
T = 2048
SLOTS = 512
Q = 128
PAGES = 64
PAGE = SLOTS // PAGES
GAIN = 512.0
HALF = SLOTS // 2
ROWS_AT = P - 16

FLOPS = 3 * 2 * 512 * Q * SLOTS


def tile_attend_bpagethensecond_s_kernel(tc, query, query2, keys_words, keys_scales, gout, vals_words, vals_scales, old, offs, out):
    nc = tc.nc
    with ExitStack() as ctx:
        keep = ctx.enter_context(tc.tile_pool(name="keep", bufs=1))
        psum = ctx.enter_context(tc.psum_pool(name="psum", bufs=1))

        def load_scales(window, scales):
            nc.vector.memset(window[:].bitcast(I32)[0:ROWS_AT, :], 0)
            nc.sync.dma_start(window[:].bitcast(I32)[ROWS_AT:P, :], scales[0].bitcast(I32))

        def place_scales(picked, name):
            plane = keep.tile([P, SLOTS], U8, align_bytes=64, name=name)
            for quad in range(4):
                nc.sync.dma_start(
                    plane[:].bitcast(I32)[32 * quad : 32 * quad + 4, :],
                    picked[:].bitcast(I32)[ROWS_AT + 4 * quad : ROWS_AT + 4 * quad + 4, :],
                )
            return plane

        def load_words(window, words):
            nc.sync.dma_start(window[:], words[0].rearrange("p t r -> p (t r)").bitcast(I32))

        def load_rows(raw, rows):
            nc.sync.dma_start(raw[:], rows.rearrange("(p j) w -> p j w", j=PACK))

        def quantize(raw, name):
            grouped = keep.tile([P, Q, PACK], BF16, align_bytes=64, name=name + "_grouped")
            nc.scalar.copy(grouped[:], raw[:].rearrange("p j w -> p w j"))
            codes = keep.tile([P, Q], U32, align_bytes=64, name=name + "_codes")
            plane = keep.tile([P, Q], U8, align_bytes=64, name=name + "_plane")
            nc.vector.quantize_mx(out=codes[:].bitcast(FP8X4), scales=plane[:], in_=grouped[:].rearrange("p w j -> p (w j)"))
            return codes, plane

        def gather(window, dtype, name):
            picked = keep.tile([P, SLOTS], dtype, align_bytes=64, name=name)
            nc.vector.tensor_copy(picked[:], window.indirect(offsets[:]))
            return picked

        def product(codes, plane, words, scales, name):
            bank = psum.tile([P, words.shape[1]], F32, name=name)
            nc.tensor.matmul_mx(out=bank[:], lhsT=codes[:].bitcast(FP8X4), lhsT_scale=plane[:], rhs=words.bitcast(FP8X4), rhs_scale=scales, start=True, stop=True)
            return bank

        def by_page(ap):
            return ap.rearrange("p (g j) -> p g j", j=PAGE)

        def over_page(ap):
            return ap.unsqueeze(2).to_broadcast([P, ap.shape[1], PAGE])

        ks_window = keep.tile([P, T], U8, tag="chain_a")
        vs_window = keep.tile([P, T], U8)
        offsets = keep.tile([P, SLOTS // 16], U16)
        nc.sync.dma_start(offsets[:], offs)
        load_scales(ks_window, keys_scales)
        load_scales(vs_window, vals_scales)
        warm_in = keep.tile([P, 1], F32)
        warm_out = keep.tile([P, 1], F32)
        nc.vector.memset(warm_in[:], 0.0)
        placed = keep.tile([P, T], F32)
        nc.vector.memset(placed[:], 0.0)
        identity = keep.tile([P, P], F32)
        make_identity(nc, identity[:])

        q2_raw = keep.tile([P, PACK, Q], F32, tag="chain_b")
        load_rows(q2_raw, query2)
        kw_window = keep.tile([P, T], I32, tag="chain_c")
        load_words(kw_window, keys_words)
        q_raw = keep.tile([P, PACK, Q], F32)
        load_rows(q_raw, query)
        nc.scalar.activation(warm_out[:], warm_in[:], ACT.Exp)

        ks_rows = gather(ks_window[:], U8, "ks_rows")
        ks = place_scales(ks_rows, "ks")
        vs_rows = gather(vs_window[:], U8, "vs_rows")
        q2_codes, q2_plane = quantize(q2_raw, "q2")
        g_raw = keep.tile([P, PACK, Q], F32, tag="chain_a")
        load_rows(g_raw, gout)
        vw_window = keep.tile([P, T], I32, tag="chain_b")
        load_words(vw_window, vals_words)
        vs = place_scales(vs_rows, "vs")

        kw = keep.tile([P, SLOTS], U32, align_bytes=64)
        halves = [slice(h * HALF, (h + 1) * HALF) for h in range(2)]
        half_pages = [slice(h * HALF // PAGE, (h + 1) * HALF // PAGE) for h in range(2)]
        b = []
        for h in range(2):
            nc.vector.tensor_copy(kw[:, halves[h]], kw_window[:].bitcast(U32).indirect(offsets[:, h * HALF // 16 : (h + 1) * HALF // 16]))
            b.append(product(q2_codes, q2_plane, kw[:, halves[h]], ks[:, halves[h]], "b%d" % h))
        old_sb = keep.tile([P, T], F32, tag="chain_c")
        nc.sync.dma_start(old_sb[:], old)
        q_codes, q_plane = quantize(q_raw, "q")
        a = product(q_codes, q_plane, kw[:], ks[:], "a")
        g_codes, g_plane = quantize(g_raw, "g")

        neg_b_max = keep.tile([P, PAGES], F32)
        for h in range(2):
            nc.vector.tensor_reduce(neg_b_max[:, half_pages[h]], by_page(b[h][:]), AX.X, ALU.max, negate=True)
        b_shifted = keep.tile([P, SLOTS], F32)
        neg_a_max = keep.tile([P, 1], F32)
        for h in range(2):
            nc.vector.tensor_tensor(by_page(b_shifted[:, halves[h]]), by_page(b[h][:]), over_page(neg_b_max[:, half_pages[h]]), ALU.add)
            if h == 0:
                nc.vector.tensor_reduce(neg_a_max[:], a[:], AX.X, ALU.max, negate=True)
        z = keep.tile([P, 1], F32)
        pa = keep.tile([P, SLOTS], F32, tag="chain_a")
        nc.scalar.activation(pa[:], a[:], ACT.Exp, bias=neg_a_max[:], accum_out=z[:])
        pb = keep.tile([P, SLOTS], F32)
        nc.scalar.activation(pb[:], b_shifted[:], ACT.Exp)

        turned = psum.tile([P, P], F32)
        for t in range(4):
            nc.tensor.matmul(turned[:], lhsT=pa[:, t:SLOTS:4], rhs=identity[:], is_transpose=True, start=(t == 0), stop=(t == 3))

        c0 = []
        for h in range(2):
            vw = keep.tile([P, HALF], U32, align_bytes=64, name="vw%d" % h)
            nc.vector.tensor_copy(vw[:], vw_window[:].bitcast(U32).indirect(offsets[:, h * HALF // 16 : (h + 1) * HALF // 16]))
            c0.append(product(g_codes, g_plane, vw[:], vs[:, halves[h]], "c%d" % h))

        turned_sb = keep.tile([P, P], F32, align_bytes=64, name="vw1")
        nc.scalar.copy(turned_sb[:], turned[:])
        sa_halves = psum.tile([P, P], F32)
        nc.tensor.transpose(sa_halves[:], turned_sb[:], identity[:])

        sb = keep.tile([P, PAGES], F32, align_bytes=64, name="vw0")
        nc.vector.tensor_reduce(sb[:], by_page(pb[:]), AX.X, ALU.add)
        inv_z_tile = keep.tile([P, 1], F32, align_bytes=64, name="g_codes")
        nc.vector.reciprocal(inv_z_tile[:], z[:])
        inv_z = inv_z_tile[:]
        drr = keep.tile([P, SLOTS], F32)
        nc.vector.tensor_tensor(drr[:, halves[0]], c0[0][:], pb[:, halves[0]], ALU.mult)
        inv_sb = keep.tile([P, PAGES], F32)
        nc.vector.reciprocal(inv_sb[:], sb[:])
        nc.vector.tensor_tensor(drr[:, halves[1]], c0[1][:], pb[:, halves[1]], ALU.mult)
        page_gain = keep.tile([P, PAGES], F32)
        nc.vector.tensor_scalar(page_gain[:], inv_sb[:], inv_z, GAIN, ALU.mult, ALU.mult)
        dr = keep.tile([P, PAGES], F32)
        nc.vector.tensor_reduce(dr[:], by_page(drr[:]), AX.X, ALU.add)
        mean_gain = keep.tile([P, PAGES, 2], F32)
        nc.vector.scalar_tensor_tensor(
            mean_gain[:],
            sa_halves[:].rearrange("p (g h) -> p g h", h=2),
            inv_z,
            page_gain[:].unsqueeze(2).to_broadcast([P, PAGES, 2]),
            ALU.mult,
            ALU.mult,
        )
        page_term = keep.tile([P, PAGES], F32)
        nc.vector.tensor_tensor(page_term[:], dr[:], page_gain[:], ALU.mult)
        mean_terms = keep.tile([P, PAGES, 2], F32)
        mean = keep.tile([P, 1], F32)
        nc.vector.scalar_tensor_tensor(
            mean_terms[:],
            mean_gain[:],
            1.0,
            dr[:].unsqueeze(2).to_broadcast([P, PAGES, 2]),
            ALU.mult,
            ALU.mult,
            accum_out=mean[:],
        )
        spread = keep.tile([P, SLOTS], F32)
        nc.vector.tensor_scalar(by_page(spread[:]), over_page(page_term[:]), mean[:], None, ALU.subtract)
        nc.vector.tensor_tensor(placed[:].indirect(offsets[:]), spread[:], pa[:], ALU.mult)

        for c, (lo, hi) in enumerate(((0, 256), (256, 768), (768, 1280), (1280, 1792), (1792, 2048))):
            cols = slice(lo, hi)
            result = keep.tile([P, hi - lo], F32, name="result%d" % c)
            nc.vector.tensor_tensor(result[:], placed[:, cols], old_sb[:, cols], ALU.add)
            nc.sync.dma_start(out[:, cols], result[:])
